import numpy as np, ml_dtypes
CORES = [16,18,20,22]
N = 4
BF = ml_dtypes.bfloat16
W, P, L, SH, RO = 4096, 256, 16, 5, 4
def parts(rng):
    return (rng.integers(0, 256, (N, 8, 16, W)), rng.integers(0, W, (N, 8, 16, P)), rng.integers(0, W, (N, 8, 16, P)),
            rng.integers(500, 1300, (N, 8, 16)), rng.integers(30, 100, (N, 8, 16)))
def pack(x, r, m, t, e):
    return {"flood": np.ascontiguousarray(x.reshape(N, 128, W)).astype(np.float32).astype(BF), "riv": np.ascontiguousarray(r.reshape(N, 128, P)).astype(np.int32),
            "bord": np.ascontiguousarray(m.reshape(N, 128, P)).astype(np.int32), "th": t.reshape(N, 128, 1).astype(np.int32), "eps": e.reshape(N, 128, 1).astype(np.int32)}
def setup_inputs(rng):
    return pack(*parts(rng))
def setup_inputs_spread(rng):
    x = np.minimum((np.exp2(3 + 5.5 * rng.random((N, 8, 1, W))) * rng.random((N, 8, 16, W))).astype(np.int64), 255)
    r = (W * rng.random((N, 8, 16, P)) ** 3).astype(np.int64); m = W - 1 - (W * rng.random((N, 8, 16, P)) ** 3).astype(np.int64)
    t = np.minimum(np.exp2(7 + 5 * rng.random((N, 8, 16))).astype(np.int64), 4080); e = np.minimum(np.exp2(8 * rng.random((N, 8, 16))).astype(np.int64) - 1, 255)
    return pack(x, r, m, t, e)
def setup_inputs_ends(rng):
    x = 255 * rng.integers(0, 2, (N, 8, 16, W)); pure = 255 * rng.integers(0, 2, (N, 8, 1, W))
    kind = rng.random((N, 8)) < 0.4; kind[:, 7] = True
    x = np.where(kind[:, :, None, None], pure, x)
    k2 = (((W - 1) * (W - 1) >> SH) + 38 * (W - 1)) & (W - 1)
    x[:, 7, :, 0] = 0
    for c in (W - 1, W - 37, k2): x[:, 7, :, c] = 255
    r = (W - 1) * rng.integers(0, 2, (N, 8, 16, P)); m = (W - 1) * rng.integers(0, 2, (N, 8, 16, P))
    t = 4080 * rng.integers(0, 2, (N, 8, 16)); t[:, :, 2] = 0; t[:, :, 5] = 4080
    e = np.zeros((N, 8, 16), np.int64)
    for q in range(N):
        for g in range(8):
            n = int(rng.choice(np.array([0, 7, 8, 8, 9, 9, 16])))
            if g == 7: n = 8 + q % 2
            e[q, g, rng.permutation(16)[:n]] = 255
    for p in (1, 8, 15):
        r[:, 7, p] = np.where((np.arange(P) // L) % 2 == 0, W - 1, 0); m[:, 7, p] = W - 1; t[:, 7, p] = 4080
    for p in (0, 3, 14):
        r[:, 7, p] = W - 1; r[:, 7, p, P - 1] = 0; m[:, 7, p] = W - 1
    t[:, 7, 0] = 0; t[:, 7, 14] = 0
    r[:, 7, 10] = ((W - 1) * (np.arange(N) % 2))[:, None]; m[:, 7, 10] = W - 1; t[:, 7, 10] = 4080
    return pack(x, r, m, t, e)
def setup_inputs_corners(rng):
    x, r, m, t, e = parts(rng)
    r = np.argsort(rng.random((N, 8, 16, W)), axis=-1)[..., :P]; r = np.ascontiguousarray(r)
    kd = rng.integers(0, 7, (N, 8, 16)); kd[:, 0] = 6; kd[0::2, 3] = 0; kd[1::2, 3] = 6; kd[:, 7, 14] = 5; kd[:, 7, 15] = 2
    r[..., L] = np.where((kd == 1) | (kd == 3), r[..., 0], r[..., L])
    r[..., P - 1] = np.where((kd == 2) | (kd == 3), r[..., P - 1 - L], r[..., P - 1])
    m = np.where(rng.random((N, 8, 16, P)) < 0.3, r, m); e = np.zeros((N, 8, 16), np.int64)
    for q in range(N):
        for g in range(8):
            k = 8 if g in (0, 7) else int(rng.choice(np.array([7, 8, 8, 9]))); o = rng.permutation(16)
            x[q, g, o[:k]] = rng.integers(0, 256, (k, 1))
            n = max(0, 9 - k - int(rng.integers(0, 2))); e[q, g, o[k:k + n]] = 255
            v = x[q, g][:, r[q, g]]; s = np.min(np.add.reduce(np.abs(v[..., :P - L] - v[..., L:]), axis=0), axis=-1); c = kd[q, g]
            t[q, g] = np.where(c == 0, 0, np.where(c < 4, 1, np.where(c == 4, s, np.where(c == 5, np.minimum(s + 1, 4080), 4080))))
    return pack(x, r, m, t, e)
def setup_inputs_ties(rng):
    x = rng.integers(0, 4, (N, 8, 16, W)); r, m = rng.integers(0, W, (2, N, 8, 16, P))
    w = rng.integers(0, W, (N, 4, 1, 12)); w[..., 0] = 0; w[..., 11] = W - 1
    r[:, 1::2] = np.take_along_axis(np.broadcast_to(w, (N, 4, 16, 12)), rng.integers(0, 12, (N, 4, 16, P)), -1)
    m[:, ::2] = np.where(rng.random((N, 4, 16, P)) < 0.5, r[:, ::2], m[:, ::2])
    return pack(x, r, m, rng.integers(0, 18, (N, 8, 16)), rng.integers(0, 3, (N, 8, 16)))
def setup_inputs_far(rng):
    k = W // 16; n = W - 2 * k; pos = np.argsort(rng.random((N, 8, W)), axis=-1); o = np.argsort(pos, axis=-1)
    share = np.where(np.arange(8) % 2 == 0, 0.5, rng.choice(np.array([0.2, 0.8]), (N, 8)))
    hn = (share * n).astype(np.int64)[..., None]; high = (pos >= k) & (pos < 2 * k + hn)
    x = np.where((pos < 2 * k)[:, :, None], 0, rng.integers(0, 8, (N, 8, 16, W))); x = np.where(high[:, :, None], 255 - x, x)
    c = rng.integers(0, 2, (N, 8, 16, P)); c[:, :, ::2] = (np.arange(P) // L + rng.integers(0, 2, (N, 8, 8, 1))) % 2; c[:, :, 1::4, P - 1] = 0
    u = rng.random((N, 8, 16, P)); hn = hn[..., None]; odd = (np.arange(16) % 2 == 1)[:, None]
    mixed = np.where(c == 1, 2 * k + (u * hn).astype(np.int64), 2 * k + hn + (u * (n - hn)).astype(np.int64))
    i = np.where(odd, c * k + (u * k).astype(np.int64), mixed)
    r = np.take_along_axis(o, i.reshape(N, 8, -1), -1).reshape(N, 8, 16, P)
    i = (1 - c) * k + rng.integers(0, k, (N, 8, 16, P)); far = np.take_along_axis(o, i.reshape(N, 8, -1), -1).reshape(N, 8, 16, P)
    m = np.where(odd & (rng.random((N, 8, 16, P)) < 0.25), far, rng.integers(0, W, (N, 8, 16, P))); m[:, :, 1::4, P - 1] = far[:, :, 1::4, P - 1]
    t = rng.integers(3925, 3976, (N, 8, 16)); t[:, :, ::4] = 3929 + 4 * rng.integers(0, 12, (N, 8, 4)); t[:, :, 1::4] = 0; t[:, :, 3::4] = rng.integers(3900, 4080, (N, 8, 4))
    e = np.where(np.argsort(rng.random((N, 8, 16)), axis=-1) < 12, 254, rng.integers(247, 255, (N, 8, 16)))
    return pack(x, r, m, t, e)
def check_inputs(d):
    bad = []
    for k, lo, hi in (("flood", 0, 255), ("riv", 0, W - 1), ("bord", 0, W - 1), ("th", 0, 4080), ("eps", 0, 255)):
        v = np.asarray(d[k]).astype(np.float64)
        if not (np.all(v >= lo) and np.all(v <= hi)): bad.append("range of " + k)
        elif not np.all(v == np.floor(v)): bad.append("whole numbers in " + k)
    return bad
def columns(x, names):
    return np.take(x, names + W * np.arange(8)[:, None, None], axis=0)
def total(v):
    return np.add.reduce(v, axis=-1, dtype=np.int16)
def reference(flood, riv, bord, th, eps):
    R = riv.astype(np.int64).reshape(N, 8, 16, P); M = bord.astype(np.int64).reshape(N, 8, 16, P); A = np.zeros((N, 8, 16), np.int64)
    T = th.astype(np.int64).reshape(N, 8, 16); E = eps.astype(np.int16).reshape(N, 8, 1, 1, 16)
    X = [np.ascontiguousarray(a.astype(np.float32).astype(np.int16).reshape(8, 16, W).transpose(0, 2, 1)).reshape(8 * W, 16) for a in flood]
    place = np.arange(P)
    for t in range(RO):
        first = np.zeros((N, 8, 16), np.int64); loops = np.zeros((N, 8, 16, L), np.int64)
        for q in range(N):
            r, m = R[q], M[q]; h = r[..., :P - 1]; x = columns(X[q], r); nxt = x[:, :, 1:]; now = np.abs(x[:, :, :P - 1] - nxt)
            before = np.concatenate([r[..., :1], r[..., :P - 2]], axis=-1)
            cand = np.stack([((h * a >> SH) + 37 * h + a + 77 * t) & (W - 1) for a in (before, r[..., 1:], m[..., :P - 1], m[..., 1:])] + [m[..., :P - 1]])
            score = np.stack([total(np.abs(columns(X[q], c) - nxt)) for c in cand])
            best = np.take_along_axis(cand, np.argmin(score, axis=0)[None], 0)[0]
            near = total((np.abs(columns(X[q], best) - nxt) < now).astype(np.int16))
            R[q, :, :, :P - 1] = np.where(near >= 9, best, h)
            x = columns(X[q], R[q]); ok = total(np.abs(x[:, :, :P - L] - x[:, :, L:])) < (T[q] + 16 * A[q])[..., None]
            first[q] = np.where(np.any(ok, axis=-1), np.argmax(ok, axis=-1), P)
            loops[q] = np.take_along_axis(R[q], np.minimum(first[q] + 1, P - L)[..., None] + np.arange(L), -1)
        for q in range(N):
            src = (q - 1 - t % (N - 1)) % N
            lp = np.where((first[src] < P)[..., None], loops[src], loops[q])
            R[q] = np.take_along_axis(np.concatenate([R[q], lp], axis=-1), place + L * (place > first[q][..., None]), -1)
            A[q] = A[q] + (first[q] < P)
            near = total((np.abs(columns(X[q], R[q]) - columns(X[q], M[q])) <= E[q]).astype(np.int16))
            M[q] = np.where(near >= 9, R[q], M[q])
    return {"yr": R.reshape(N, 128, P).astype(np.float32), "ym": M.reshape(N, 128, P).astype(np.float32), "ya": A.reshape(N, 128, 1).astype(np.float32)}

@@ -1,0 +1,692 @@
+from concourse.mybir import AluOpType, AxisListType, ActivationFunctionType
+
+A_ = AluOpType
+F_ = ActivationFunctionType
+BND = [0, 128, 256]
+SC = 1024
+NSP = [2, 2]
+TUNE = {'R2': (20, 'S'), 'FR2': (40, 'V'), 'L00': (-20, '.'), 'K0': (-10, '.'), 'A0': (10, '.'), 'C12': (20, '.'), 'R1': (0, 'S'),
+        'C02': (0, 'V'), 'C10': (-40, 'V'), 'Q11': (80, '.'), 'C11': (20, '.'), 'P01': (0, 'S'), 'FA2': (30, '.'), 'N0': (40, '.'),
+        'FA1': (-40, '.'), 'FA0': (80, '.'), 'M2': (0, 'S'), 'N1': (40, '.'), 'C00': (-30, '.'), 'C13': (-10, '.'), 'FR1': (0, 'S'),
+        'FR0': (40, '.'), 'C14': (-40, '.'), 'C03': (0, 'S'), 'Q00': (20, '.'), 'E01': (20, '.'), '': (-80, '.'), 'C04': (-20, '.'),
+        'L11': (-10, '.'), 'M0': (-40, '.')}
+WIN = 0.0
+NEARS = [(1, 1)]
+NA = 2
+PEC = 0.45
+RO = 4
+CY = 0.83
+GC = 1.5
+LAT = 70.0
+NCH = len(BND) - 1
+
+SCRATCH = {
+    "X": ("sbuf", [128, 4096], "bfloat16"), "RI": ("sbuf", [128, 256], "int32"), "BI": ("sbuf", [128, 256], "int32"),
+    "TI": ("sbuf", [128, 1], "int32"), "EI": ("sbuf", [128, 1], "int32"), "EPF": ("sbuf", [128, 1], "float32"),
+    "THR": ("sbuf", [128, 1], "float32"), "AC": ("sbuf", [128, 1], "float32"), "CNT": ("sbuf", [128, 1], "float32"),
+    "RN": ("sbuf", [128, 256], "float32"), "MN": ("sbuf", [128, 256], "float32"),
+    "YR": ("sbuf", [128, 272], "float32"), "YM": ("sbuf", [128, 272], "float32"),
+    "RU": ("sbuf", [128, 256], "uint16"), "MU": ("sbuf", [128, 256], "uint16"), "PU": ("sbuf", [128, 256], "uint16"),
+    "RP": ("sbuf", [128, 296], "float32"),
+    "GR": ("sbuf", [128, 4112], "bfloat16"), "GM": ("sbuf", [128, 4096], "bfloat16"), "GP": ("sbuf", [128, 4096], "bfloat16"),
+    "AB": ("sbuf", [128, 3840], "bfloat16"), "NW": ("sbuf", [128, 4096], "bfloat16"), "A3": ("sbuf", [128, 4096], "bfloat16"),
+    "I3": ("sbuf", [128, 4096], "bfloat16"), "NR": ("sbuf", [128, 4096], "bfloat16"),
+    "DM": ("sbuf", [128, 256], "float32"), "DDN": ("sbuf", [128, 256], "float32"), "RM": ("sbuf", [128, 256], "float32"),
+    "BIGC": ("sbuf", [128, 256], "float32"), "IOB": ("sbuf", [128, 128], "bfloat16"), "CMD": ("sbuf", [128, 256], "float32"),
+    "DIAG": ("sbuf", [128, 256], "float32"), "SEG": ("sbuf", [128, 256], "float32"), "IK": ("sbuf", [128, 16], "float32"),
+    "PI": ("sbuf", [128, 1], "int32"), "PF": ("sbuf", [128, 1], "float32"),
+    "ZT": ("sbuf", [128, 144], "bfloat16"), "IP": ("sbuf", [128, 128], "bfloat16"), "IN": ("sbuf", [128, 128], "bfloat16"),
+    "OFF": ("sbuf", [128, 16], "uint16"), "LG": ("sbuf", [128, 256], "float32"), "LS": ("sbuf", [128, 256], "float32"),
+    "LPI": ("sbuf", [128, 16], "int32"), "LD": ("sbuf", [128, 16], "float32"),
+    "KB0": ("psum", [128, 512], "float32"), "KB1": ("psum", [128, 512], "float32"), "CB": ("psum", [128, 512], "float32"),
+    "NB": ("psum", [128, 512], "float32"), "XW": ("psum", [128, 512], "float32"),
+    "SB0": ("psum", [128, 512], "float32"), "SB1": ("psum", [128, 512], "float32"), "SB2": ("psum", [128, 512], "float32"),
+}
+for _k in range(NCH):
+    _n = BND[_k + 1] - BND[_k]
+    SCRATCH["CI%d" % _k] = ("sbuf", [128, 4 * _n], "int32")
+    SCRATCH["CU%d" % _k] = ("sbuf", [128, 4 * _n], "uint16")
+    SCRATCH["DS%d" % _k] = ("sbuf", [128, 64 * _n], "bfloat16")
+    SCRATCH["DA%d" % _k] = ("sbuf", [128, 80 * _n], "bfloat16")
+    SCRATCH["KM%d" % _k] = ("sbuf", [128, _n], "float32")
+    SCRATCH["KI%d" % _k] = ("sbuf", [128, _n], "int32")
+    SCRATCH["MI%d" % _k] = ("sbuf", [128, _n], "int32")
+    SCRATCH["FI%d" % _k] = ("sbuf", [128, _n], "float32")
+    SCRATCH["OU%d" % _k] = ("sbuf", [128, _n], "uint16")
+    SCRATCH["DD%d" % _k] = ("sbuf", [128, _n], "float32")
+    SCRATCH["CM%d" % _k] = ("sbuf", [128, 4 * _n], "bfloat16")
+for _k in range(RO):
+    SCRATCH["SEND%d" % _k] = ("sbuf", [128, 16], "float32")
+    SCRATCH["LAND%d" % _k] = ("sbuf", [128, 16], "float32")
+LOADS = ["RI", "BI", "X", "TI", "EI"]
+OUTS = ["yr", "ym", "ya"]
+SEMAPHORES = (["qV", "qS", "qP", "qG"] + ["ld" + n for n in LOADS] + ["st" + n for n in OUTS]
+              + ["arr%d" % t for t in range(RO)] + ["snt%d" % t for t in range(RO)])
+PSUM = [n for n in SCRATCH if SCRATCH[n][0] == "psum"]
+POOL = ["SB0", "SB1", "SB2"]
+
+
+def sl(T, r):
+    return T[r[0]][:, r[1]:r[2]]
+
+
+def build_ops():
+    ops = []
+    seen = {}
+    cur = [""]
+
+    def O(engs, fn, R, W, **kw):
+        op = dict(kw, engs=engs, fn=fn, R=list(R), W=list(W), preds={}, i=len(ops), grp=cur[0])
+        for rd, lst in ((True, op["R"]), (False, op["W"])):
+            for (b, c0, c1) in lst:
+                if b == "POOL":
+                    continue
+                ws, rs = seen.setdefault(b, ([], []))
+                for (x0, x1, q) in ws:
+                    if x0 < c1 and c0 < x1:
+                        op["preds"][q["i"]] = 1
+                if not rd:
+                    for (x0, x1, q) in rs:
+                        if x0 < c1 and c0 < x1:
+                            op["preds"][q["i"]] = 1
+        for (b, c0, c1) in op["R"]:
+            if b != "POOL":
+                seen[b][1].append((c0, c1, op))
+        for (b, c0, c1) in op["W"]:
+            if b != "POOL":
+                ws, rs = seen[b]
+                ws[:] = [w for w in ws if not (c0 <= w[0] and w[1] <= c1)] + [(c0, c1, op)]
+                rs[:] = [w for w in rs if not (c0 <= w[0] and w[1] <= c1) or w[2] is op]
+        op["preds"].pop(op["i"], None)
+        ops.append(op)
+        return op
+
+    def vt(n, c):
+        return 55 + CY * max(64, n * c)
+
+    def tt(o, a, b, alu, cost=None):
+        n = o[2] - o[1]
+        if cost is None:
+            cost = 1 if (a[0] in PSUM or b[0] in PSUM) else 2
+        return O({"V": vt(n, cost)}, lambda e, g, T, op: g.vector.tensor_tensor(sl(T, o), sl(T, a), sl(T, b), alu), [a, b], [o])
+
+    def tsc(o, a, s1, s2, op0, op1=None, cost=1, sreads=()):
+        n = o[2] - o[1]
+
+        def fn(e, g, T, op):
+            v1 = sl(T, s1) if isinstance(s1, tuple) else s1
+            v2 = sl(T, s2) if isinstance(s2, tuple) else s2
+            if op1 is None:
+                return g.vector.tensor_scalar(sl(T, o), sl(T, a), v1, None, op0)
+            return g.vector.tensor_scalar(sl(T, o), sl(T, a), v1, v2, op0, op1)
+        rd = [a] + [s for s in (s1, s2) if isinstance(s, tuple)]
+        return O({"V": vt(n, cost)}, fn, rd, [o])
+
+    def copy(o, a, both=False):
+        n = o[2] - o[1]
+        engs = {"V": vt(n, 1)}
+        if both:
+            engs["S"] = 70 + CY * n
+
+        def fn(e, g, T, op):
+            if e == "V":
+                return g.vector.tensor_copy(sl(T, o), sl(T, a))
+            return g.scalar.activation(sl(T, o), sl(T, a), F_.Copy)
+        return O(engs, fn, [a], [o])
+
+    def affine(o, a, mul, add):
+        n = o[2] - o[1]
+
+        def fn(e, g, T, op):
+            if e == "V":
+                if mul == 1.0:
+                    return g.vector.tensor_scalar(sl(T, o), sl(T, a), add, None, A_.add)
+                return g.vector.tensor_scalar(sl(T, o), sl(T, a), mul, add, A_.mult, A_.add)
+            return g.scalar.activation(sl(T, o), sl(T, a), F_.Copy, bias=add, scale=mul)
+        return O({"V": vt(n, 1), "S": 70 + CY * n}, fn, [a], [o])
+
+    def memset(o, v):
+        return O({"V": vt(o[2] - o[1], 0.5)}, lambda e, g, T, op: g.vector.memset(sl(T, o), v), [], [o])
+
+    def gather(o, win, off, only=None):
+        n = o[2] - o[1]
+        engs = {"V": 50 + GC * CY * n, "S": 65 + GC * CY * n}
+        if only:
+            engs = {only: engs[only]}
+
+        def fn(e, g, T, op):
+            src = sl(T, win).indirect(sl(T, off))
+            if e == "V":
+                return g.vector.tensor_copy(sl(T, o), src)
+            return g.scalar.activation(sl(T, o), src, F_.Copy)
+        return O(engs, fn, [win, off], [o])
+
+    def gather_tt(o, win, off, b, alu):
+        n = o[2] - o[1]
+        return O({"V": 50 + GC * CY * n}, lambda e, g, T, op: g.vector.tensor_tensor(sl(T, o), sl(T, win).indirect(sl(T, off)), sl(T, b), alu),
+                 [win, off, b], [o])
+
+    def signdiff(o, a, b):
+        absdiff(o, a, b, F_.Sign, -0.5)
+
+    def absdiff(o, a, b, func=F_.Abs, bias=0.0):
+        tot = o[2] - o[1]
+        nb = (tot + 511) // 512
+        w = -(-tot // nb)
+        w = -(-w // 16) * 16
+        for c in range(0, tot, w):
+            m = min(w, tot - c)
+            a1 = (a[0], a[1] + c, a[1] + c + m)
+            b1 = (b[0], b[1] + c, b[1] + c + m)
+            o1 = (o[0], o[1] + c, o[1] + c + m)
+
+            def sub(e, g, T, op, a1=a1, b1=b1, m=m):
+                d = T[op["bank"]][:, 0:m]
+                g.tensor.matmul(d, T.IP[:], sl(T, a1), True, False)
+                return g.tensor.matmul(d, T.IN[:], sl(T, b1), False, True)
+            q = O({"P": 2 * 0.45 * max(64, m) + 30}, sub, [a1, b1, ("IP", 0, 128), ("IN", 0, 128)], [("POOL", 0, m)], alloc=True)
+            r = O({"S": 70 + CY * m}, lambda e, g, T, op, o1=o1, m=m: g.scalar.activation(sl(T, o1), T[op["src"]["bank"]][:, 0:m], func, bias=bias),
+                  [("POOL", 0, m)], [o1], src=q)
+            r["preds"][q["i"]] = 1
+
+    def cand_abs(o, win, off, b, ds):
+        tot = o[2] - o[1]
+
+        def fn(e, g, T, op):
+            src = sl(T, win).indirect(sl(T, off))
+            if e == "V":
+                return g.vector.tensor_tensor(sl(T, ds), src, sl(T, b), A_.subtract)
+            return g.scalar.activation(sl(T, ds), src, F_.Copy)
+        G = O({"V": 50 + GC * CY * tot, "S": 65 + GC * CY * tot}, fn, [win, off, b], [ds])
+        G["subs"], G["abss"] = [], []
+        nb = (tot + 511) // 512
+        w = -(-tot // nb)
+        w = -(-w // 16) * 16
+        for c in range(0, tot, w):
+            m = min(w, tot - c)
+            a1 = (ds[0], ds[1] + c, ds[1] + c + m)
+            b1 = (b[0], b[1] + c, b[1] + c + m)
+            o1 = (o[0], o[1] + c, o[1] + c + m)
+
+            def sub(e, g, T, op, a1=a1, b1=b1, m=m):
+                d = T[op["bank"]][:, 0:m]
+                g.tensor.matmul(d, T.IP[:], sl(T, a1), True, False)
+                return g.tensor.matmul(d, T.IN[:], sl(T, b1), False, True)
+            q = O({"P": 2 * 0.45 * max(64, m) + 30}, sub, [a1, b1, ("IP", 0, 128), ("IN", 0, 128)], [("POOL", 0, m)], alloc=True)
+
+            def ab(e, g, T, op, o1=o1, m=m):
+                if op.get("whole"):
+                    return g.scalar.activation(sl(T, o), sl(T, ds), F_.Abs)
+                return g.scalar.activation(sl(T, o1), T[op["src"]["bank"]][:, 0:m], F_.Abs)
+            r = O({"S": 70 + CY * m}, ab, [ds, ("POOL", 0, m)], [o if c == 0 else o1], src=q, wdur=70 + CY * tot)
+            r["preds"][q["i"]] = 1
+            G["subs"].append(q["i"])
+            G["abss"].append(r["i"])
+        for x in G["abss"][1:]:
+            ops[x]["preds"].pop(G["abss"][0], None)
+
+    def stage_sum(o, a, tag=None):
+        n = o[2] - o[1]
+
+        def fn(e, g, T, op):
+            d = sl(T, o)
+            r = None
+            for x in tag or []:
+                g.tensor.matmul(d, T.IP[:], sl(T, x), x is tag[0], False)
+            for p in range(16):
+                r = g.tensor.matmul(d, T.ZT[:, 15 - p:143 - p], T[a[0]][:, a[1] + p:a[2]:16], tag is None and p == 0, p == 15)
+            return r
+        rd = [a, ("ZT", 0, 144)] + (tag + [("IP", 0, 128)] if tag is not None else [])
+        O({"P": (16 + len(tag or [])) * 0.45 * max(64, n) + 30}, fn, rd, [o])
+
+    def load(dst, src, w, ns):
+        O({"Y": ns}, lambda e, g, T, op: g.sync.dma_start(T[dst][:], T[src][:]), [], [(dst, 0, w)], sem="ld" + dst)
+    load("RI", "riv", 256, 2000)
+    load("X", "flood", 4096, 7000)
+    load("BI", "bord", 256, 2500)
+    load("TI", "th", 1, 2500)
+    load("EI", "eps", 1, 2500)
+
+    def gop(fn, ns, R, W):
+        O({"G": ns}, fn, R, W)
+
+    def sel(buf, n, pattern, base, cm, cmp):
+        gop(lambda e, g, T, op: g.affine_select(T[buf][:], T[buf][:], pattern, cmp, 0.0, base, cm), 170 + 2 * CY * n, [(buf, 0, n)], [(buf, 0, n)])
+    memset(("ZT", 0, 144), float(SC))
+    memset(("IP", 0, 128), 1.0)
+    sel("IP", 128, [[-1, 128]], 0, 1, A_.is_equal)
+    sel("ZT", 144, [[0, 9], [1, 16]], -15, 0, A_.is_equal)
+    sel("ZT", 144, [[-16, 9], [0, 16]], 0, 1, A_.is_ge)
+    sel("ZT", 144, [[16, 9], [0, 16]], 15, -1, A_.is_ge)
+    gop(lambda e, g, T, op: g.iota(T.PI[:], [[0, 1]], 0, 1), 140, [], [("PI", 0, 1)])
+    gop(lambda e, g, T, op: g.iota(T.IOB[:], [[1, 128]], 0, 0, allow_small_or_imprecise_dtypes=True), 350, [], [("IOB", 0, 128)])
+    gop(lambda e, g, T, op: g.iota(T.CMD[:], [[0, 16], [1, 16]], 0, 0, allow_small_or_imprecise_dtypes=True), 560, [], [("CMD", 0, 256)])
+    gop(lambda e, g, T, op: g.iota(T.IK[:], [[1, 16]], 256, 0, allow_small_or_imprecise_dtypes=True), 160, [], [("IK", 0, 16)])
+    tsc(("IN", 0, 128), ("IP", 0, 128), -1.0, None, A_.mult)
+    tsc(("PI", 0, 1), ("PI", 0, 1), 15, None, A_.bitwise_and)
+    copy(("PF", 0, 1), ("PI", 0, 1))
+    tsc(("DIAG", 0, 256), ("CMD", 0, 256), ("PF", 0, 1), None, A_.is_equal)
+    tsc(("SEG", 0, 256), ("CMD", 0, 256), 0.5, None, A_.is_gt)
+    memset(("BIGC", 0, 256), 1.0e7)
+    memset(("NW", 4080, 4096), 0.0)
+    memset(("GR", 4096, 4112), 0.0)
+    memset(("YR", 264, 272), 0.0)
+    memset(("YM", 256, 272), 0.0)
+    memset(("RP", 264, 296), -4096.0)
+    memset(("NB", 240, 257), 1.0e7)
+    memset(("NB", 256, 257), 0.0)
+    memset(("AC", 0, 1), 0.0)
+    for k in range(NCH):
+        n = BND[k + 1] - BND[k]
+        for m in range(1, 5):
+            memset(("CM%d" % k, (m - 1) * n, m * n), float(m * n))
+
+    XWIN = ("X", 0, 4096)
+    TB = [0] + [b + 2 for b in BND[1:-1]] + [240, 256]
+    NT = len(TB) - 1
+
+    def first_names(ta, tb):
+        tsc(("RU", ta, tb), ("RI", ta, tb), 0, None, A_.add)
+        copy(("RN", ta, tb), ("RI", ta, tb))
+
+    def names_side(t, ta, tb, kind):
+        if kind == "R":
+            gather(("GR", 16 * ta, 16 * tb), XWIN, ("RU", ta, tb))
+            affine(("XW", ta, tb), ("RN", ta, tb), 1.0, 32.0)
+            affine(("YR", 8 + ta, 8 + tb), ("RN", ta, tb), 1.0, -2912.0)
+            if ta == 0:
+                affine(("YR", 7, 8), ("RN", 0, 1), 1.0, -2912.0)
+            affine(("XW", 256 + ta, 256 + tb), ("RN", ta, tb), 128.0, 2912.0 + 77.0 * t)
+        else:
+            affine(("YM", ta, tb), ("MN", ta, tb), 1.0, -2912.0)
+            gather(("GM", 16 * ta, 16 * tb), XWIN, ("MU", ta, tb))
+
+    def accretion(ta, tb, last):
+        absdiff(("A3", 16 * ta, 16 * tb), ("GR", 16 * ta, 16 * tb), ("GM", 16 * ta, 16 * tb))
+        tsc(("I3", 16 * ta, 16 * tb), ("A3", 16 * ta, 16 * tb), ("EPF", 0, 1), None, A_.is_le, cost=0.5)
+        c = ("CB", ta, tb)
+        stage_sum(c, ("I3", 16 * ta, 16 * tb))
+        mn = ("MN", ta, tb)
+        tt(("DM", ta, tb), ("RN", ta, tb), mn, A_.subtract)
+        tsc(c, c, 8.5 * SC, None, A_.is_gt)
+        tt(c, c, ("DM", ta, tb), A_.mult)
+        tt(mn, c, mn, A_.add)
+        if not last:
+            copy(("MU", ta, tb), mn)
+
+    def cand_lists(k, half):
+        a, b = BND[k], BND[k + 1]
+        n = b - a
+        ci = "CI%d" % k
+        lo, hi = (0, 2 * n) if half == 0 else (2 * n, 4 * n)
+        other = [("YR", 7 + a, 7 + b), ("YR", 9 + a, 9 + b)] if half == 0 else [("YM", a, b), ("YM", a + 1, b + 1)]
+        for q in range(2):
+            tt((ci, lo + q * n, lo + q * n + n), ("XW", a, b), other[q], A_.mult)
+        tsc((ci, lo, hi), (ci, lo, hi), 5, None, A_.arith_shift_right)
+        for q in range(2):
+            r = (ci, lo + q * n, lo + q * n + n)
+            tt(r, ("XW", 256 + a, 256 + b), r, A_.add)
+        tsc((ci, lo, hi), (ci, lo, hi), 4095, None, A_.bitwise_and)
+        copy(("CU%d" % k, lo, hi), (ci, lo, hi))
+
+    def kreg(k, m):
+        n = BND[k + 1] - BND[k]
+        if m == 4:
+            return ("CB", 256 + BND[k], 256 + BND[k] + n)
+        return ("KB%d" % (k % 2), m * n, m * n + n)
+
+    def key(k, m):
+        n = BND[k + 1] - BND[k]
+        stage_sum(kreg(k, m), ("DA%d" % k, 16 * n * m, 16 * n * (m + 1)),
+                  [("IOB", 0, n)] + ([("CM%d" % k, (m - 1) * n, m * n)] if m else []))
+
+    def cand_heights(k, m):
+        a, b = BND[k], BND[k + 1]
+        n = b - a
+        nxt = ("GR", 16 * a + 16, 16 * b + 16)
+        da = ("DA%d" % k, 16 * n * m, 16 * n * (m + 1))
+        if m < 4:
+            ds = ("DS%d" % k, 16 * n * m, 16 * n * (m + 1))
+            cand_abs(da, XWIN, ("CU%d" % k, m * n, m * n + n), nxt, ds)
+        else:
+            absdiff(da, ("GM", 16 * a, 16 * b), nxt)
+        key(k, m)
+
+    def choose(k):
+        a, b = BND[k], BND[k + 1]
+        n = b - a
+        kb = "KB%d" % (k % 2)
+        cur[0] = "K%d" % k
+        km, ki = ("KM%d" % k, 0, n), ("KI%d" % k, 0, n)
+        order = [4, 0, 1, 2, 3]
+        copy(km, kreg(k, order[0]), both=True)
+        for m in order[1:]:
+            tt(ki if m == order[-1] else km, kreg(k, m), km, A_.min)
+        tsc(("MI%d" % k, 0, n), ki, SC - 1, None, A_.bitwise_and)
+        tsc(("OU%d" % k, 0, n), ("MI%d" % k, 0, n), 16.0, ("PF", 0, 1), A_.mult, A_.add)
+        ps = [a + n * q // NSP[k] for q in range(NSP[k] + 1)]
+        cur[0] = "E%d" % k
+        for x, y in zip(ps, ps[1:]):
+            nr, win, off = ("NR", 16 * x, 16 * y), ("DA%d" % k, 0, 80 * n), ("OU%d" % k, x - a, y - a)
+            cur[0] = "E%d%d" % (k, ps.index(x))
+            if (k, ps.index(x)) in NEARS:
+                gather(nr, win, off, "S")
+                signdiff(nr, ("NW", 16 * x, 16 * y), nr)
+            else:
+                gather_tt(nr, win, off, ("NW", 16 * x, 16 * y), A_.is_lt)
+            stage_sum(("CB", x, y), nr)
+        dd = ("DD%d" % k, 0, n)
+        cur[0] = "D%d" % k
+        for m in range(5):
+            r = kreg(k, m)
+            tt(r, r, ki, A_.is_equal)
+        tt((kb, 0, 4 * n), (kb, 0, 4 * n), ("CI%d" % k, 0, 4 * n), A_.mult)
+        r = kreg(k, 4)
+        tt(r, r, ("MN", a, b), A_.mult)
+        tt(dd, (kb, 0, n), ("RN", a, b), A_.subtract)
+        for m in range(1, 5):
+            tt(dd, kreg(k, m), dd, A_.add)
+        for x, y in zip(ps, ps[1:]):
+            cur[0] = "P%d%d" % (k, ps.index(x))
+            c = ("CB", x, y)
+            tsc(c, c, (1.0 if (k, ps.index(x)) in NEARS else 8.5) * SC, None, A_.is_gt)
+            tt(c, c, (dd[0], x - a, y - a), A_.mult)
+            rp = ("RP", 8 + x, 8 + y)
+            tt(rp, c, ("RN", x, y), A_.add)
+            copy(("PU", x, y), rp)
+            gather(("GP", 16 * x, 16 * y), XWIN, ("PU", x, y))
+
+    def necks(na, nb, last):
+        absdiff(("AB", 16 * na, 16 * nb), ("GP", 16 * na, 16 * nb), ("GP", 16 * na + 256, 16 * nb + 256))
+        stage_sum(("NB", na, nb), ("AB", 16 * na, 16 * nb))
+        tt(("DDN", na, nb), ("RP", 24 + na, 24 + nb), ("RP", 8 + na, 8 + nb), A_.subtract)
+        hi = 255 if last else nb
+        n = hi - na
+        ini = ("RM", na - 1, na) if na else 1.0e7
+        rd = [("NB", na, hi), ("BIGC", na, hi)] + ([ini] if na else [])
+        O({"V": vt(n, 1)}, lambda e, g, T, op: g.vector.tensor_tensor_scan(T.RM[:, na:hi], T.NB[:, na:hi], T.BIGC[:, na:hi],
+            sl(T, ini) if na else 1.0e7, A_.min, A_.min), rd, [("RM", na, hi)])
+        tsc(("NB", 257 + na, 257 + hi), ("RM", na, hi), ("THR", 0, 1), None, A_.is_lt)
+
+    def shift(ta, tb, last):
+        m = ("NB", ta, tb)
+        tt(m, ("NB", 256 + ta, 256 + tb), ("DDN", ta, tb), A_.mult)
+        tt(("RN", ta, tb), m, ("RP", 8 + ta, 8 + tb), A_.add)
+        copy(("RU", ta, tb), ("RN", ta, tb))
+
+    def loops(t):
+        O({"V": vt(256, 1)}, lambda e, g, T, op: g.vector.tensor_reduce(T.CNT[:], T.NB[:, 256:512], AxisListType.X, A_.add),
+          [("NB", 256, 512)], [("CNT", 0, 1)])
+        tsc(("OFF", 0, 16), ("IK", 0, 16), ("CNT", 0, 1), None, A_.subtract)
+        gather_tt(("LG", 0, 256), ("RP", 8, 296), ("OFF", 0, 16), ("DIAG", 0, 256), A_.mult)
+        O({"V": vt(256, 1)}, lambda e, g, T, op: g.vector.tensor_tensor_scan(T.LS[:], T.SEG[:], T.LG[:], 0.0, A_.mult, A_.add),
+          [("SEG", 0, 256), ("LG", 0, 256)], [("LS", 0, 256)])
+        s = "SEND%d" % t
+        O({"V": vt(16, 1)}, lambda e, g, T, op: g.vector.tensor_scalar(T[s][:], T.LS[:, 15:256:16], 4096.0, None, A_.add),
+          [("LS", 0, 256)], [(s, 0, 16)])
+        snd = O({"G": 1500}, None, [(s, 0, 16)], [], send=t)
+        tsc(("AC", 0, 1), ("NB", 511, 512), ("AC", 0, 1), None, A_.add)
+        tsc(("THR", 0, 1), ("NB", 511, 512), 16.0 * SC, ("THR", 0, 1), A_.mult, A_.add)
+        return snd
+
+    def loop_in(t, snd, last):
+        q = O({"V": vt(16, 2)}, lambda e, g, T, op: g.vector.tensor_tensor(T.LPI[:], T["LAND%d" % t][:], T.LS[:, 15:256:16], A_.max),
+              [("LS", 0, 256)], [("LPI", 0, 16)], ext="arr%d" % t)
+        q["preds"][snd["i"]] = 1
+        tsc(("LPI", 0, 16), ("LPI", 0, 16), 4095, None, A_.bitwise_and)
+        tt(("LD", 0, 16), ("LPI", 0, 16), ("RP", 248, 264), A_.subtract)
+        tt(("LD", 0, 16), ("NB", 496, 512), ("LD", 0, 16), A_.mult)
+        tt(("RN", 240, 256), ("LD", 0, 16), ("RP", 248, 264), A_.add)
+        copy(("RU", 240, 256), ("RN", 240, 256))
+
+    for i in range(NT):
+        first_names(TB[i], TB[i + 1])
+    copy(("MN", 0, 256), ("BI", 0, 256))
+    copy(("MU", 0, 256), ("BI", 0, 256))
+    copy(("EPF", 0, 1), ("EI", 0, 1))
+    tsc(("THR", 0, 1), ("TI", 0, 1), float(SC), None, A_.mult)
+    for t in range(RO):
+        for i in range(NT):
+            ta, tb = TB[i], TB[i + 1]
+            cur[0] = "R%d" % i
+            names_side(t, ta, tb, "R")
+            if i >= NA - 1 and i < NT - 1:
+                continue
+            if i == NT - 1:
+                ta = TB[NA - 1]
+            if t:
+                cur[0] = "A%d" % i
+                accretion(ta, tb, False)
+            cur[0] = "M%d" % i
+            names_side(t, ta, tb, "M")
+        for k in range(NCH):
+            a, b = BND[k], BND[k + 1]
+            cur[0] = "L%d0" % k
+            cand_lists(k, 0)
+            cur[0] = "L%d1" % k
+            cand_lists(k, 1)
+            hi = min(16 * b, 4080)
+            for m in (4, 0, 1, 2, 3):
+                cur[0] = "C%d%d" % (k, m)
+                cand_heights(k, m)
+            cur[0] = "N%d" % k
+            absdiff(("NW", 16 * a, hi), ("GR", 16 * a, hi), ("GR", 16 * a + 16, hi + 16))
+            choose(k)
+            for q in range(NSP[k]):
+                x, y = a + (b - a) * q // NSP[k], a + (b - a) * (q + 1) // NSP[k]
+                cur[0] = "Q%d%d" % (k, q)
+                necks(x - 16 if x else 0, y - 16, y == 256)
+        cur[0] = "O"
+        snd = loops(t)
+        for i in range(NT - 1):
+            cur[0] = "S%d" % i
+            shift(TB[i], TB[i + 1], t == RO - 1)
+        cur[0] = "I"
+        loop_in(t, snd, t == RO - 1)
+    for i in range(NT):
+        ta, tb = TB[i], TB[i + 1]
+        cur[0] = "FR%d" % i
+        gather(("GR", 16 * ta, 16 * tb), XWIN, ("RU", ta, tb))
+        cur[0] = "FA%d" % i
+        accretion(ta, tb, True)
+
+    def store(dst, src, w):
+        O({"Y": 2000}, lambda e, g, T, op: g.sync.dma_start(T[dst][:], T[src][:, 0:w]), [(src, 0, w)], [], sem="st" + dst)
+    store("ya", "AC", 1)
+    store("yr", "RN", 256)
+    store("ym", "MN", 256)
+    return ops
+
+
+def schedule(ops):
+    n = len(ops)
+    succ = [[] for _ in range(n)]
+    left = [0] * n
+    for op in ops:
+        for p in op["preds"]:
+            succ[p].append(op["i"])
+            left[op["i"]] += 1
+    prio = [0.0] * n
+    free = {e: 0.0 for e in "VSPGY"}
+    fin = [0.0] * n
+    bank = {}
+    pool = {b: None for b in POOL}
+    ready = [i for i in range(n) if left[i] == 0]
+    order = []
+    choice = {}
+    for op in ops:
+        off, ch = TUNE.get(op["grp"], (0, "."))
+        prio[op["i"]] = -(op["i"] + off)
+        if len(op["engs"]) > 1 and ch in op["engs"] and max(op["engs"].values()) > 300:
+            choice[op["i"]] = ch
+
+    def done(i, f):
+        fin[i] = f
+        for q in succ[i]:
+            left[q] -= 1
+            if left[q] == 0:
+                if ops[q].get("null"):
+                    done(q, max([fin[p] for p in ops[q]["preds"]]))
+                else:
+                    ready.append(q)
+
+    for op in ops:
+        op["bk"] = sorted({r[0] for r in op["R"] + op["W"] if r[0] in PSUM})
+
+    while ready:
+        best = None
+        found = []
+        for i in ready:
+            op = ops[i]
+            t0 = 0.0
+            for p in op["preds"]:
+                x = fin[p] + LAT + (1500 if "send" in ops[p] else 0)
+                t0 = max(t0, x)
+            bk = None
+            if op.get("alloc"):
+                opts = [(fin[c] + LAT if c is not None else 0.0, b) for b, c in pool.items() if c != -1]
+                if not opts:
+                    continue
+                x, bk = min(opts)
+                t0 = max(t0, x)
+            cand = None
+            for e, d in op["engs"].items():
+                if choice.get(i, e) != e:
+                    continue
+                s = max(t0, free[e])
+                for b in op["bk"]:
+                    for f, (x, q) in bank.get(b, {}).items():
+                        if f != e:
+                            s = max(s, x + LAT)
+                if cand is None or s + d < cand[0]:
+                    cand = (s + d, s, e)
+            ef, s, e = cand
+            found.append((s, i, e, ef, bk))
+            if best is None or s < best[0]:
+                best = found[-1]
+        s0, e0 = best[0] + WIN, best[2]
+        for x in found:
+            if x[2] == e0 and x[0] <= s0 and prio[x[1]] > prio[best[1]]:
+                best = x
+        s, i, e, ef, bk = best
+        op = ops[i]
+        if "subs" in op and e == "V":
+            for x in op["subs"] + op["abss"][1:]:
+                ops[x]["null"] = True
+            z = ops[op["abss"][0]]
+            z["whole"] = True
+            z["engs"] = {"S": z["wdur"]}
+        ready.remove(i)
+        op["eng"] = e
+        op["deps"] = list(op["preds"])
+        if op.get("alloc"):
+            op["bank"] = bk
+            if pool[bk] is not None:
+                op["deps"].append(pool[bk])
+            pool[bk] = -1
+        if "src" in op and not op.get("whole"):
+            pool[op["src"]["bank"]] = i
+        for b in op["bk"]:
+            d = bank.setdefault(b, {})
+            for f, (x, q) in d.items():
+                if f != e:
+                    op["deps"].append(q)
+            d[e] = (ef, i)
+        op["start"] = s
+        free[e] = s + 60.0 if e == "Y" else ef
+        order.append(i)
+        done(i, ef)
+    return order, max(fin)
+
+
+def make_plan():
+    ops = build_ops()
+    order, span = schedule(ops)
+    know = {e: {} for e in "VSPGY"}
+    cnt = {"V": 0, "S": 0, "P": 0, "G": 0}
+    out = []
+    for i in order:
+        op = ops[i]
+        e = op["eng"]
+        need = {}
+        srcs = []
+        deps = list(op["deps"])
+        for d in deps:
+            q = ops[d]
+            if q.get("null"):
+                deps.extend(x for x in q["preds"] if x not in deps)
+                continue
+            if "send" in q:
+                if "ext" in op:
+                    need[op["ext"]] = "ARR"
+                continue
+            sem, v = q["tok"]
+            if know[e].get(sem, 0) < v:
+                srcs.append((v, sem, q))
+        srcs.sort(key=lambda x: -x[2]["pos"])
+        for v, sem, q in srcs:
+            if know[e].get(sem, 0) >= v:
+                continue
+            need[sem] = max(need.get(sem, 0), v)
+            know[e][sem] = v
+            for s2, v2 in q["clk"].items():
+                if know[e].get(s2, 0) < v2:
+                    know[e][s2] = v2
+        op["waits"] = need
+        op["clk"] = dict(know[e])
+        op["pos"] = len(out)
+        if "sem" in op:
+            op["tok"] = (op["sem"], 16)
+        elif "send" in op:
+            op["tok"] = None
+        else:
+            cnt[e] += 1
+            op["tok"] = ("q" + e, cnt[e])
+        out.append(op)
+    return out, cnt, span
+
+
+CACHE = {}
+
+
+def rank_program(g, core, T, topo):
+    rank = T.rank_of(core)
+    if rank is None:
+        return
+    if "plan" not in CACHE:
+        CACHE["plan"] = make_plan()
+    plan, cnt, span = CACHE["plan"]
+    N = len(T.cores)
+    hand = {"V": g.vector, "S": g.scalar, "P": g.tensor, "G": g, "Y": g.sync}
+
+    def link(src, dst):
+        return topo.engines(src, dst)[:4]
+
+    for op in plan:
+        e = op["eng"]
+        h = hand[e]
+        for sem, v in op["waits"].items():
+            if v == "ARR":
+                t = int(sem[3:])
+                v = len(link(T.cores[(rank - 1 - t % (N - 1)) % N], core))
+            h.wait_ge(T.sem[sem], v)
+        if "send" in op:
+            t = op["send"]
+            dst = T.cores[(rank + 1 + t % (N - 1)) % N]
+            rid, pid, _s = topo.addr(dst)
+            mask = 0
+            for x in link(core, dst):
+                mask |= 1 << x
+            g.remote_dma(T["LAND%d" % t][:], T["SEND%d" % t][:], T.sem["arr%d" % t], T.sem["snt%d" % t], pid, rid, mask)
+            continue
+        ins = op["fn"](e, g, T, op)
+        sem, v = op["tok"]
+        ins.then_inc(T.sem[sem], 16 if "sem" in op else 1)
+    for t in range(RO):
+        g.wait_ge(T.sem["snt%d" % t], len(link(core, T.cores[(rank + 1 + t % (N - 1)) % N])))
+    for e in "VSPG":
+        g.wait_ge(T.sem["q" + e], cnt[e])
+    for n in LOADS:
+        g.sync.wait_ge(T.sem["ld" + n], 16)
+    for n in OUTS:
+        g.sync.wait_ge(T.sem["st" + n], 16)

@@ -4,16 +4,13 @@ A_ = AluOpType
 F_ = ActivationFunctionType
 BND = [0, 128, 256]
 SC = 1024
-NSP = [2, 2]
-TUNE = {'R2': (20, 'S'), 'FR2': (40, 'V'), 'L00': (-20, '.'), 'K0': (-10, '.'), 'A0': (10, '.'), 'C12': (20, '.'), 'R1': (0, 'S'),
-        'C02': (0, 'V'), 'C10': (-40, 'V'), 'Q11': (80, '.'), 'C11': (20, '.'), 'P01': (0, 'S'), 'FA2': (30, '.'), 'N0': (40, '.'),
-        'FA1': (-40, '.'), 'FA0': (80, '.'), 'M2': (0, 'S'), 'N1': (40, '.'), 'C00': (-30, '.'), 'C13': (-10, '.'), 'FR1': (0, 'S'),
-        'FR0': (40, '.'), 'C14': (-40, '.'), 'C03': (0, 'S'), 'Q00': (20, '.'), 'E01': (20, '.'), '': (-80, '.'), 'C04': (-20, '.'),
-        'L11': (-10, '.'), 'M0': (-40, '.')}
+NSP = [1, 2]
+TBP = [0, 66, 130, 240, 256]
+TUNE = {'R2': (10, '.'), 'FR2': (420, 'S'), 'L00': (0, '.'), 'K0': (40, '.'), 'A0': (-35, '.'), 'C12': (120, '.'), 'R1': (-100, '.'), 'C02': (55, '.'), 'C10': (-140, '.'), 'Q11': (165, '.'), 'C11': (30, '.'), 'P01': (0, 'S'), 'FA2': (20, '.'), 'N0': (20, '.'), 'FA1': (-340, '.'), 'FA0': (205, '.'), 'M2': (0, 'S'), 'N1': (130, '.'), 'C00': (-85, 'V'), 'C13': (-30, 'V'), 'FR1': (195, 'V'), 'FR0': (-35, '.'), 'C14': (-105, '.'), 'C03': (30, '.'), 'Q00': (195, '.'), 'E01': (20, '.'), '': (55, '.'), 'C04': (-170, '.'), 'L11': (-40, '.'), 'M0': (-70, 'V'), 'R3': (-85, 'V'), 'P11': (-205, 'S'), 'P10': (-315, 'V'), 'L01': (35, '.'), 'M3': (-150, 'S'), 'R0': (45, 'V'), 'O': (-270, '.'), 'Q10': (-5, '.'), 'P00': (55, 'S'), 'FR3': (-110, 'V'), 'C01': (30, 'S'), 'E10': (30, '.'), 'M1': (40, '.'), 'D0': (-235, '.'), 'A1': (-5, '.'), 'S1': (-100, '.'), 'A3': (-55, '.'), 'S0': (-175, '.'), 'E00': (175, '.'), 'E11': (120, '.'), 'S2': (-5, '.'), 'I': (-95, '.'), 'L10': (-40, '.'), 'FA3': (-35, '.'), 'D1': (5, '.'), 'K1': (-95, '.')}
 WIN = 0.0
 NEARS = [(1, 1)]
-NA = 2
-PEC = 0.45
+NA = 3
+PEC = 0.46
 RO = 4
 CY = 0.83
 GC = 1.5
@@ -39,8 +36,8 @@ SCRATCH = {
     "OFF": ("sbuf", [128, 16], "uint16"), "LG": ("sbuf", [128, 256], "float32"), "LS": ("sbuf", [128, 256], "float32"),
     "LPI": ("sbuf", [128, 16], "int32"), "LD": ("sbuf", [128, 16], "float32"),
     "KB0": ("psum", [128, 512], "float32"), "KB1": ("psum", [128, 512], "float32"), "CB": ("psum", [128, 512], "float32"),
-    "NB": ("psum", [128, 512], "float32"), "XW": ("psum", [128, 512], "float32"),
-    "SB0": ("psum", [128, 512], "float32"), "SB1": ("psum", [128, 512], "float32"), "SB2": ("psum", [128, 512], "float32"),
+    "NB": ("psum", [128, 512], "float32"),
+    "SB0": ("psum", [128, 1024], "float32"), "SB1": ("psum", [128, 1024], "float32"),
 }
 for _k in range(NCH):
     _n = BND[_k + 1] - BND[_k]
@@ -63,7 +60,8 @@ OUTS = ["yr", "ym", "ya"]
 SEMAPHORES = (["qV", "qS", "qP", "qG"] + ["ld" + n for n in LOADS] + ["st" + n for n in OUTS]
               + ["arr%d" % t for t in range(RO)] + ["snt%d" % t for t in range(RO)])
 PSUM = [n for n in SCRATCH if SCRATCH[n][0] == "psum"]
-POOL = ["SB0", "SB1", "SB2"]
+POOL = ["SB0", "SB1"]
+BW = 1024
 
 
 def sl(T, r):
@@ -166,25 +164,31 @@ def build_ops():
         return O({"V": 50 + GC * CY * n}, lambda e, g, T, op: g.vector.tensor_tensor(sl(T, o), sl(T, win).indirect(sl(T, off)), sl(T, b), alu),
                  [win, off, b], [o])
 
+    def blocks(o, a, b):
+        tot = o[2] - o[1]
+        w = -(-tot // ((tot + BW - 1) // BW))
+        w = -(-w // 32) * 32
+        for c in range(0, tot, w):
+            m = min(w, tot - c)
+            yield [(x[0], x[1] + c, x[1] + c + m) for x in (o, a, b)] + [m]
+
+    def sub_op(a1, b1, m):
+        def sub(e, g, T, op):
+            r = None
+            for x in range(0, m, 512):
+                y = min(x + 512, m)
+                d = T[op["bank"]][:, x:y]
+                g.tensor.matmul(d, T.IP[:], T[a1[0]][:, a1[1] + x:a1[1] + y], True, False)
+                r = g.tensor.matmul(d, T.IN[:], T[b1[0]][:, b1[1] + x:b1[1] + y], False, True)
+            return r
+        return O({"P": 2 * PEC * max(64, m) + 30}, sub, [a1, b1, ("IP", 0, 128), ("IN", 0, 128)], [("POOL", 0, m)], alloc=True)
+
     def signdiff(o, a, b):
         absdiff(o, a, b, F_.Sign, -0.5)
 
     def absdiff(o, a, b, func=F_.Abs, bias=0.0):
-        tot = o[2] - o[1]
-        nb = (tot + 511) // 512
-        w = -(-tot // nb)
-        w = -(-w // 16) * 16
-        for c in range(0, tot, w):
-            m = min(w, tot - c)
-            a1 = (a[0], a[1] + c, a[1] + c + m)
-            b1 = (b[0], b[1] + c, b[1] + c + m)
-            o1 = (o[0], o[1] + c, o[1] + c + m)
-
-            def sub(e, g, T, op, a1=a1, b1=b1, m=m):
-                d = T[op["bank"]][:, 0:m]
-                g.tensor.matmul(d, T.IP[:], sl(T, a1), True, False)
-                return g.tensor.matmul(d, T.IN[:], sl(T, b1), False, True)
-            q = O({"P": 2 * 0.45 * max(64, m) + 30}, sub, [a1, b1, ("IP", 0, 128), ("IN", 0, 128)], [("POOL", 0, m)], alloc=True)
+        for o1, a1, b1, m in blocks(o, a, b):
+            q = sub_op(a1, b1, m)
             r = O({"S": 70 + CY * m}, lambda e, g, T, op, o1=o1, m=m: g.scalar.activation(sl(T, o1), T[op["src"]["bank"]][:, 0:m], func, bias=bias),
                   [("POOL", 0, m)], [o1], src=q)
             r["preds"][q["i"]] = 1
@@ -199,20 +203,9 @@ def build_ops():
             return g.scalar.activation(sl(T, ds), src, F_.Copy)
         G = O({"V": 50 + GC * CY * tot, "S": 65 + GC * CY * tot}, fn, [win, off, b], [ds])
         G["subs"], G["abss"] = [], []
-        nb = (tot + 511) // 512
-        w = -(-tot // nb)
-        w = -(-w // 16) * 16
-        for c in range(0, tot, w):
-            m = min(w, tot - c)
-            a1 = (ds[0], ds[1] + c, ds[1] + c + m)
-            b1 = (b[0], b[1] + c, b[1] + c + m)
-            o1 = (o[0], o[1] + c, o[1] + c + m)
-
-            def sub(e, g, T, op, a1=a1, b1=b1, m=m):
-                d = T[op["bank"]][:, 0:m]
-                g.tensor.matmul(d, T.IP[:], sl(T, a1), True, False)
-                return g.tensor.matmul(d, T.IN[:], sl(T, b1), False, True)
-            q = O({"P": 2 * 0.45 * max(64, m) + 30}, sub, [a1, b1, ("IP", 0, 128), ("IN", 0, 128)], [("POOL", 0, m)], alloc=True)
+        for o1, a1, b1, m in blocks(o, ds, b):
+            c = o1[1] - o[1]
+            q = sub_op(a1, b1, m)
 
             def ab(e, g, T, op, o1=o1, m=m):
                 if op.get("whole"):
@@ -237,7 +230,7 @@ def build_ops():
                 r = g.tensor.matmul(d, T.ZT[:, 15 - p:143 - p], T[a[0]][:, a[1] + p:a[2]:16], tag is None and p == 0, p == 15)
             return r
         rd = [a, ("ZT", 0, 144)] + (tag + [("IP", 0, 128)] if tag is not None else [])
-        O({"P": (16 + len(tag or [])) * 0.45 * max(64, n) + 30}, fn, rd, [o])
+        O({"P": (16 + len(tag or [])) * PEC * max(64, n) + 30}, fn, rd, [o])
 
     def load(dst, src, w, ns):
         O({"Y": ns}, lambda e, g, T, op: g.sync.dma_start(T[dst][:], T[src][:]), [], [(dst, 0, w)], sem="ld" + dst)
@@ -273,8 +266,6 @@ def build_ops():
     memset(("YR", 264, 272), 0.0)
     memset(("YM", 256, 272), 0.0)
     memset(("RP", 264, 296), -4096.0)
-    memset(("NB", 240, 257), 1.0e7)
-    memset(("NB", 256, 257), 0.0)
     memset(("AC", 0, 1), 0.0)
     for k in range(NCH):
         n = BND[k + 1] - BND[k]
@@ -282,7 +273,7 @@ def build_ops():
             memset(("CM%d" % k, (m - 1) * n, m * n), float(m * n))
 
     XWIN = ("X", 0, 4096)
-    TB = [0] + [b + 2 for b in BND[1:-1]] + [240, 256]
+    TB = TBP
     NT = len(TB) - 1
 
     def first_names(ta, tb):
@@ -292,11 +283,11 @@ def build_ops():
     def names_side(t, ta, tb, kind):
         if kind == "R":
             gather(("GR", 16 * ta, 16 * tb), XWIN, ("RU", ta, tb))
-            affine(("XW", ta, tb), ("RN", ta, tb), 1.0, 32.0)
+            affine(("NB", ta, tb), ("RN", ta, tb), 1.0, 32.0)
             affine(("YR", 8 + ta, 8 + tb), ("RN", ta, tb), 1.0, -2912.0)
             if ta == 0:
                 affine(("YR", 7, 8), ("RN", 0, 1), 1.0, -2912.0)
-            affine(("XW", 256 + ta, 256 + tb), ("RN", ta, tb), 128.0, 2912.0 + 77.0 * t)
+            affine(("NB", 256 + ta, 256 + tb), ("RN", ta, tb), 128.0, 2912.0 + 77.0 * t)
         else:
             affine(("YM", ta, tb), ("MN", ta, tb), 1.0, -2912.0)
             gather(("GM", 16 * ta, 16 * tb), XWIN, ("MU", ta, tb))
@@ -321,11 +312,11 @@ def build_ops():
         lo, hi = (0, 2 * n) if half == 0 else (2 * n, 4 * n)
         other = [("YR", 7 + a, 7 + b), ("YR", 9 + a, 9 + b)] if half == 0 else [("YM", a, b), ("YM", a + 1, b + 1)]
         for q in range(2):
-            tt((ci, lo + q * n, lo + q * n + n), ("XW", a, b), other[q], A_.mult)
+            tt((ci, lo + q * n, lo + q * n + n), ("NB", a, b), other[q], A_.mult)
         tsc((ci, lo, hi), (ci, lo, hi), 5, None, A_.arith_shift_right)
         for q in range(2):
             r = (ci, lo + q * n, lo + q * n + n)
-            tt(r, ("XW", 256 + a, 256 + b), r, A_.add)
+            tt(r, ("NB", 256 + a, 256 + b), r, A_.add)
         tsc((ci, lo, hi), (ci, lo, hi), 4095, None, A_.bitwise_and)
         copy(("CU%d" % k, lo, hi), (ci, lo, hi))
 
@@ -475,6 +466,9 @@ def build_ops():
             for q in range(NSP[k]):
                 x, y = a + (b - a) * q // NSP[k], a + (b - a) * (q + 1) // NSP[k]
                 cur[0] = "Q%d%d" % (k, q)
+                if y == 256:
+                    memset(("NB", 240, 255), 1.0e7)
+                    memset(("NB", 256, 257), 0.0)
                 necks(x - 16 if x else 0, y - 16, y == 256)
         cur[0] = "O"
         snd = loops(t)

from concourse.mybir import AluOpType, AxisListType, ActivationFunctionType

A_ = AluOpType
F_ = ActivationFunctionType
BND = [0, 128, 256]
SC = 1024
NSP = [1, 2]
TBP = [0, 66, 130, 240, 256]
TUNE = {'R2': (10, '.'), 'FR2': (420, 'S'), 'L00': (0, '.'), 'K0': (40, '.'), 'A0': (-35, '.'), 'C12': (120, '.'), 'R1': (-100, '.'), 'C02': (55, '.'), 'C10': (-140, '.'), 'Q11': (165, '.'), 'C11': (30, '.'), 'P01': (0, 'S'), 'FA2': (20, '.'), 'N0': (20, '.'), 'FA1': (-340, '.'), 'FA0': (205, '.'), 'M2': (0, 'S'), 'N1': (130, '.'), 'C00': (-85, 'V'), 'C13': (-30, 'V'), 'FR1': (195, 'V'), 'FR0': (-35, '.'), 'C14': (-105, '.'), 'C03': (30, '.'), 'Q00': (195, '.'), 'E01': (20, '.'), '': (55, '.'), 'C04': (-170, '.'), 'L11': (-40, '.'), 'M0': (-70, 'V'), 'R3': (-85, 'V'), 'P11': (-205, 'S'), 'P10': (-315, 'V'), 'L01': (35, '.'), 'M3': (-150, 'S'), 'R0': (45, 'V'), 'O': (-270, '.'), 'Q10': (-5, '.'), 'P00': (55, 'S'), 'FR3': (-110, 'V'), 'C01': (30, 'S'), 'E10': (30, '.'), 'M1': (40, '.'), 'D0': (-235, '.'), 'A1': (-5, '.'), 'S1': (-100, '.'), 'A3': (-55, '.'), 'S0': (-175, '.'), 'E00': (175, '.'), 'E11': (120, '.'), 'S2': (-5, '.'), 'I': (-95, '.'), 'L10': (-40, '.'), 'FA3': (-35, '.'), 'D1': (5, '.'), 'K1': (-95, '.')}
WIN = 0.0
NEARS = [(1, 1)]
NA = 3
PEC = 0.46
RO = 4
CY = 0.83
GC = 1.5
LAT = 70.0
NCH = len(BND) - 1

SCRATCH = {
    "X": ("sbuf", [128, 4096], "bfloat16"), "RI": ("sbuf", [128, 256], "int32"), "BI": ("sbuf", [128, 256], "int32"),
    "TI": ("sbuf", [128, 1], "int32"), "EI": ("sbuf", [128, 1], "int32"), "EPF": ("sbuf", [128, 1], "float32"),
    "THR": ("sbuf", [128, 1], "float32"), "AC": ("sbuf", [128, 1], "float32"), "CNT": ("sbuf", [128, 1], "float32"),
    "RN": ("sbuf", [128, 256], "float32"), "MN": ("sbuf", [128, 256], "float32"),
    "YR": ("sbuf", [128, 272], "float32"), "YM": ("sbuf", [128, 272], "float32"),
    "RU": ("sbuf", [128, 256], "uint16"), "MU": ("sbuf", [128, 256], "uint16"), "PU": ("sbuf", [128, 256], "uint16"),
    "RP": ("sbuf", [128, 296], "float32"),
    "GR": ("sbuf", [128, 4112], "bfloat16"), "GM": ("sbuf", [128, 4096], "bfloat16"), "GP": ("sbuf", [128, 4096], "bfloat16"),
    "AB": ("sbuf", [128, 3840], "bfloat16"), "NW": ("sbuf", [128, 4096], "bfloat16"), "A3": ("sbuf", [128, 4096], "bfloat16"),
    "I3": ("sbuf", [128, 4096], "bfloat16"), "NR": ("sbuf", [128, 4096], "bfloat16"),
    "DM": ("sbuf", [128, 256], "float32"), "DDN": ("sbuf", [128, 256], "float32"), "RM": ("sbuf", [128, 256], "float32"),
    "BIGC": ("sbuf", [128, 256], "float32"), "IOB": ("sbuf", [128, 128], "bfloat16"), "CMD": ("sbuf", [128, 256], "float32"),
    "DIAG": ("sbuf", [128, 256], "float32"), "SEG": ("sbuf", [128, 256], "float32"), "IK": ("sbuf", [128, 16], "float32"),
    "PI": ("sbuf", [128, 1], "int32"), "PF": ("sbuf", [128, 1], "float32"),
    "ZT": ("sbuf", [128, 144], "bfloat16"), "IP": ("sbuf", [128, 128], "bfloat16"), "IN": ("sbuf", [128, 128], "bfloat16"),
    "OFF": ("sbuf", [128, 16], "uint16"), "LG": ("sbuf", [128, 256], "float32"), "LS": ("sbuf", [128, 256], "float32"),
    "LPI": ("sbuf", [128, 16], "int32"), "LD": ("sbuf", [128, 16], "float32"),
    "KB0": ("psum", [128, 512], "float32"), "KB1": ("psum", [128, 512], "float32"), "CB": ("psum", [128, 512], "float32"),
    "NB": ("psum", [128, 512], "float32"),
    "SB0": ("psum", [128, 1024], "float32"), "SB1": ("psum", [128, 1024], "float32"),
}
for _k in range(NCH):
    _n = BND[_k + 1] - BND[_k]
    SCRATCH["CI%d" % _k] = ("sbuf", [128, 4 * _n], "int32")
    SCRATCH["CU%d" % _k] = ("sbuf", [128, 4 * _n], "uint16")
    SCRATCH["DS%d" % _k] = ("sbuf", [128, 64 * _n], "bfloat16")
    SCRATCH["DA%d" % _k] = ("sbuf", [128, 80 * _n], "bfloat16")
    SCRATCH["KM%d" % _k] = ("sbuf", [128, _n], "float32")
    SCRATCH["KI%d" % _k] = ("sbuf", [128, _n], "int32")
    SCRATCH["MI%d" % _k] = ("sbuf", [128, _n], "int32")
    SCRATCH["FI%d" % _k] = ("sbuf", [128, _n], "float32")
    SCRATCH["OU%d" % _k] = ("sbuf", [128, _n], "uint16")
    SCRATCH["DD%d" % _k] = ("sbuf", [128, _n], "float32")
    SCRATCH["CM%d" % _k] = ("sbuf", [128, 4 * _n], "bfloat16")
for _k in range(RO):
    SCRATCH["SEND%d" % _k] = ("sbuf", [128, 16], "float32")
    SCRATCH["LAND%d" % _k] = ("sbuf", [128, 16], "float32")
LOADS = ["RI", "BI", "X", "TI", "EI"]
OUTS = ["yr", "ym", "ya"]
SEMAPHORES = (["qV", "qS", "qP", "qG"] + ["ld" + n for n in LOADS] + ["st" + n for n in OUTS]
              + ["arr%d" % t for t in range(RO)] + ["snt%d" % t for t in range(RO)])
PSUM = [n for n in SCRATCH if SCRATCH[n][0] == "psum"]
POOL = ["SB0", "SB1"]
BW = 1024


def sl(T, r):
    return T[r[0]][:, r[1]:r[2]]


def build_ops():
    ops = []
    seen = {}
    cur = [""]

    def O(engs, fn, R, W, **kw):
        op = dict(kw, engs=engs, fn=fn, R=list(R), W=list(W), preds={}, i=len(ops), grp=cur[0])
        for rd, lst in ((True, op["R"]), (False, op["W"])):
            for (b, c0, c1) in lst:
                if b == "POOL":
                    continue
                ws, rs = seen.setdefault(b, ([], []))
                for (x0, x1, q) in ws:
                    if x0 < c1 and c0 < x1:
                        op["preds"][q["i"]] = 1
                if not rd:
                    for (x0, x1, q) in rs:
                        if x0 < c1 and c0 < x1:
                            op["preds"][q["i"]] = 1
        for (b, c0, c1) in op["R"]:
            if b != "POOL":
                seen[b][1].append((c0, c1, op))
        for (b, c0, c1) in op["W"]:
            if b != "POOL":
                ws, rs = seen[b]
                ws[:] = [w for w in ws if not (c0 <= w[0] and w[1] <= c1)] + [(c0, c1, op)]
                rs[:] = [w for w in rs if not (c0 <= w[0] and w[1] <= c1) or w[2] is op]
        op["preds"].pop(op["i"], None)
        ops.append(op)
        return op

    def vt(n, c):
        return 55 + CY * max(64, n * c)

    def tt(o, a, b, alu, cost=None):
        n = o[2] - o[1]
        if cost is None:
            cost = 1 if (a[0] in PSUM or b[0] in PSUM) else 2
        return O({"V": vt(n, cost)}, lambda e, g, T, op: g.vector.tensor_tensor(sl(T, o), sl(T, a), sl(T, b), alu), [a, b], [o])

    def tsc(o, a, s1, s2, op0, op1=None, cost=1, sreads=()):
        n = o[2] - o[1]

        def fn(e, g, T, op):
            v1 = sl(T, s1) if isinstance(s1, tuple) else s1
            v2 = sl(T, s2) if isinstance(s2, tuple) else s2
            if op1 is None:
                return g.vector.tensor_scalar(sl(T, o), sl(T, a), v1, None, op0)
            return g.vector.tensor_scalar(sl(T, o), sl(T, a), v1, v2, op0, op1)
        rd = [a] + [s for s in (s1, s2) if isinstance(s, tuple)]
        return O({"V": vt(n, cost)}, fn, rd, [o])

    def copy(o, a, both=False):
        n = o[2] - o[1]
        engs = {"V": vt(n, 1)}
        if both:
            engs["S"] = 70 + CY * n

        def fn(e, g, T, op):
            if e == "V":
                return g.vector.tensor_copy(sl(T, o), sl(T, a))
            return g.scalar.activation(sl(T, o), sl(T, a), F_.Copy)
        return O(engs, fn, [a], [o])

    def affine(o, a, mul, add):
        n = o[2] - o[1]

        def fn(e, g, T, op):
            if e == "V":
                if mul == 1.0:
                    return g.vector.tensor_scalar(sl(T, o), sl(T, a), add, None, A_.add)
                return g.vector.tensor_scalar(sl(T, o), sl(T, a), mul, add, A_.mult, A_.add)
            return g.scalar.activation(sl(T, o), sl(T, a), F_.Copy, bias=add, scale=mul)
        return O({"V": vt(n, 1), "S": 70 + CY * n}, fn, [a], [o])

    def memset(o, v):
        return O({"V": vt(o[2] - o[1], 0.5)}, lambda e, g, T, op: g.vector.memset(sl(T, o), v), [], [o])

    def gather(o, win, off, only=None):
        n = o[2] - o[1]
        engs = {"V": 50 + GC * CY * n, "S": 65 + GC * CY * n}
        if only:
            engs = {only: engs[only]}

        def fn(e, g, T, op):
            src = sl(T, win).indirect(sl(T, off))
            if e == "V":
                return g.vector.tensor_copy(sl(T, o), src)
            return g.scalar.activation(sl(T, o), src, F_.Copy)
        return O(engs, fn, [win, off], [o])

    def gather_tt(o, win, off, b, alu):
        n = o[2] - o[1]
        return O({"V": 50 + GC * CY * n}, lambda e, g, T, op: g.vector.tensor_tensor(sl(T, o), sl(T, win).indirect(sl(T, off)), sl(T, b), alu),
                 [win, off, b], [o])

    def blocks(o, a, b):
        tot = o[2] - o[1]
        w = -(-tot // ((tot + BW - 1) // BW))
        w = -(-w // 32) * 32
        for c in range(0, tot, w):
            m = min(w, tot - c)
            yield [(x[0], x[1] + c, x[1] + c + m) for x in (o, a, b)] + [m]

    def sub_op(a1, b1, m):
        def sub(e, g, T, op):
            r = None
            for x in range(0, m, 512):
                y = min(x + 512, m)
                d = T[op["bank"]][:, x:y]
                g.tensor.matmul(d, T.IP[:], T[a1[0]][:, a1[1] + x:a1[1] + y], True, False)
                r = g.tensor.matmul(d, T.IN[:], T[b1[0]][:, b1[1] + x:b1[1] + y], False, True)
            return r
        return O({"P": 2 * PEC * max(64, m) + 30}, sub, [a1, b1, ("IP", 0, 128), ("IN", 0, 128)], [("POOL", 0, m)], alloc=True)

    def signdiff(o, a, b):
        absdiff(o, a, b, F_.Sign, -0.5)

    def absdiff(o, a, b, func=F_.Abs, bias=0.0):
        for o1, a1, b1, m in blocks(o, a, b):
            q = sub_op(a1, b1, m)
            r = O({"S": 70 + CY * m}, lambda e, g, T, op, o1=o1, m=m: g.scalar.activation(sl(T, o1), T[op["src"]["bank"]][:, 0:m], func, bias=bias),
                  [("POOL", 0, m)], [o1], src=q)
            r["preds"][q["i"]] = 1

    def cand_abs(o, win, off, b, ds):
        tot = o[2] - o[1]

        def fn(e, g, T, op):
            src = sl(T, win).indirect(sl(T, off))
            if e == "V":
                return g.vector.tensor_tensor(sl(T, ds), src, sl(T, b), A_.subtract)
            return g.scalar.activation(sl(T, ds), src, F_.Copy)
        G = O({"V": 50 + GC * CY * tot, "S": 65 + GC * CY * tot}, fn, [win, off, b], [ds])
        G["subs"], G["abss"] = [], []
        for o1, a1, b1, m in blocks(o, ds, b):
            c = o1[1] - o[1]
            q = sub_op(a1, b1, m)

            def ab(e, g, T, op, o1=o1, m=m):
                if op.get("whole"):
                    return g.scalar.activation(sl(T, o), sl(T, ds), F_.Abs)
                return g.scalar.activation(sl(T, o1), T[op["src"]["bank"]][:, 0:m], F_.Abs)
            r = O({"S": 70 + CY * m}, ab, [ds, ("POOL", 0, m)], [o if c == 0 else o1], src=q, wdur=70 + CY * tot)
            r["preds"][q["i"]] = 1
            G["subs"].append(q["i"])
            G["abss"].append(r["i"])
        for x in G["abss"][1:]:
            ops[x]["preds"].pop(G["abss"][0], None)

    def stage_sum(o, a, tag=None):
        n = o[2] - o[1]

        def fn(e, g, T, op):
            d = sl(T, o)
            r = None
            for x in tag or []:
                g.tensor.matmul(d, T.IP[:], sl(T, x), x is tag[0], False)
            for p in range(16):
                r = g.tensor.matmul(d, T.ZT[:, 15 - p:143 - p], T[a[0]][:, a[1] + p:a[2]:16], tag is None and p == 0, p == 15)
            return r
        rd = [a, ("ZT", 0, 144)] + (tag + [("IP", 0, 128)] if tag is not None else [])
        O({"P": (16 + len(tag or [])) * PEC * max(64, n) + 30}, fn, rd, [o])

    def load(dst, src, w, ns):
        O({"Y": ns}, lambda e, g, T, op: g.sync.dma_start(T[dst][:], T[src][:]), [], [(dst, 0, w)], sem="ld" + dst)
    load("RI", "riv", 256, 2000)
    load("X", "flood", 4096, 7000)
    load("BI", "bord", 256, 2500)
    load("TI", "th", 1, 2500)
    load("EI", "eps", 1, 2500)

    def gop(fn, ns, R, W):
        O({"G": ns}, fn, R, W)

    def sel(buf, n, pattern, base, cm, cmp):
        gop(lambda e, g, T, op: g.affine_select(T[buf][:], T[buf][:], pattern, cmp, 0.0, base, cm), 170 + 2 * CY * n, [(buf, 0, n)], [(buf, 0, n)])
    memset(("ZT", 0, 144), float(SC))
    memset(("IP", 0, 128), 1.0)
    sel("IP", 128, [[-1, 128]], 0, 1, A_.is_equal)
    sel("ZT", 144, [[0, 9], [1, 16]], -15, 0, A_.is_equal)
    sel("ZT", 144, [[-16, 9], [0, 16]], 0, 1, A_.is_ge)
    sel("ZT", 144, [[16, 9], [0, 16]], 15, -1, A_.is_ge)
    gop(lambda e, g, T, op: g.iota(T.PI[:], [[0, 1]], 0, 1), 140, [], [("PI", 0, 1)])
    gop(lambda e, g, T, op: g.iota(T.IOB[:], [[1, 128]], 0, 0, allow_small_or_imprecise_dtypes=True), 350, [], [("IOB", 0, 128)])
    gop(lambda e, g, T, op: g.iota(T.CMD[:], [[0, 16], [1, 16]], 0, 0, allow_small_or_imprecise_dtypes=True), 560, [], [("CMD", 0, 256)])
    gop(lambda e, g, T, op: g.iota(T.IK[:], [[1, 16]], 256, 0, allow_small_or_imprecise_dtypes=True), 160, [], [("IK", 0, 16)])
    tsc(("IN", 0, 128), ("IP", 0, 128), -1.0, None, A_.mult)
    tsc(("PI", 0, 1), ("PI", 0, 1), 15, None, A_.bitwise_and)
    copy(("PF", 0, 1), ("PI", 0, 1))
    tsc(("DIAG", 0, 256), ("CMD", 0, 256), ("PF", 0, 1), None, A_.is_equal)
    tsc(("SEG", 0, 256), ("CMD", 0, 256), 0.5, None, A_.is_gt)
    memset(("BIGC", 0, 256), 1.0e7)
    memset(("NW", 4080, 4096), 0.0)
    memset(("GR", 4096, 4112), 0.0)
    memset(("YR", 264, 272), 0.0)
    memset(("YM", 256, 272), 0.0)
    memset(("RP", 264, 296), -4096.0)
    memset(("AC", 0, 1), 0.0)
    for k in range(NCH):
        n = BND[k + 1] - BND[k]
        for m in range(1, 5):
            memset(("CM%d" % k, (m - 1) * n, m * n), float(m * n))

    XWIN = ("X", 0, 4096)
    TB = TBP
    NT = len(TB) - 1

    def first_names(ta, tb):
        tsc(("RU", ta, tb), ("RI", ta, tb), 0, None, A_.add)
        copy(("RN", ta, tb), ("RI", ta, tb))

    def names_side(t, ta, tb, kind):
        if kind == "R":
            gather(("GR", 16 * ta, 16 * tb), XWIN, ("RU", ta, tb))
            affine(("NB", ta, tb), ("RN", ta, tb), 1.0, 32.0)
            affine(("YR", 8 + ta, 8 + tb), ("RN", ta, tb), 1.0, -2912.0)
            if ta == 0:
                affine(("YR", 7, 8), ("RN", 0, 1), 1.0, -2912.0)
            affine(("NB", 256 + ta, 256 + tb), ("RN", ta, tb), 128.0, 2912.0 + 77.0 * t)
        else:
            affine(("YM", ta, tb), ("MN", ta, tb), 1.0, -2912.0)
            gather(("GM", 16 * ta, 16 * tb), XWIN, ("MU", ta, tb))

    def accretion(ta, tb, last):
        absdiff(("A3", 16 * ta, 16 * tb), ("GR", 16 * ta, 16 * tb), ("GM", 16 * ta, 16 * tb))
        tsc(("I3", 16 * ta, 16 * tb), ("A3", 16 * ta, 16 * tb), ("EPF", 0, 1), None, A_.is_le, cost=0.5)
        c = ("CB", ta, tb)
        stage_sum(c, ("I3", 16 * ta, 16 * tb))
        mn = ("MN", ta, tb)
        tt(("DM", ta, tb), ("RN", ta, tb), mn, A_.subtract)
        tsc(c, c, 8.5 * SC, None, A_.is_gt)
        tt(c, c, ("DM", ta, tb), A_.mult)
        tt(mn, c, mn, A_.add)
        if not last:
            copy(("MU", ta, tb), mn)

    def cand_lists(k, half):
        a, b = BND[k], BND[k + 1]
        n = b - a
        ci = "CI%d" % k
        lo, hi = (0, 2 * n) if half == 0 else (2 * n, 4 * n)
        other = [("YR", 7 + a, 7 + b), ("YR", 9 + a, 9 + b)] if half == 0 else [("YM", a, b), ("YM", a + 1, b + 1)]
        for q in range(2):
            tt((ci, lo + q * n, lo + q * n + n), ("NB", a, b), other[q], A_.mult)
        tsc((ci, lo, hi), (ci, lo, hi), 5, None, A_.arith_shift_right)
        for q in range(2):
            r = (ci, lo + q * n, lo + q * n + n)
            tt(r, ("NB", 256 + a, 256 + b), r, A_.add)
        tsc((ci, lo, hi), (ci, lo, hi), 4095, None, A_.bitwise_and)
        copy(("CU%d" % k, lo, hi), (ci, lo, hi))

    def kreg(k, m):
        n = BND[k + 1] - BND[k]
        if m == 4:
            return ("CB", 256 + BND[k], 256 + BND[k] + n)
        return ("KB%d" % (k % 2), m * n, m * n + n)

    def key(k, m):
        n = BND[k + 1] - BND[k]
        stage_sum(kreg(k, m), ("DA%d" % k, 16 * n * m, 16 * n * (m + 1)),
                  [("IOB", 0, n)] + ([("CM%d" % k, (m - 1) * n, m * n)] if m else []))

    def cand_heights(k, m):
        a, b = BND[k], BND[k + 1]
        n = b - a
        nxt = ("GR", 16 * a + 16, 16 * b + 16)
        da = ("DA%d" % k, 16 * n * m, 16 * n * (m + 1))
        if m < 4:
            ds = ("DS%d" % k, 16 * n * m, 16 * n * (m + 1))
            cand_abs(da, XWIN, ("CU%d" % k, m * n, m * n + n), nxt, ds)
        else:
            absdiff(da, ("GM", 16 * a, 16 * b), nxt)
        key(k, m)

    def choose(k):
        a, b = BND[k], BND[k + 1]
        n = b - a
        kb = "KB%d" % (k % 2)
        cur[0] = "K%d" % k
        km, ki = ("KM%d" % k, 0, n), ("KI%d" % k, 0, n)
        order = [4, 0, 1, 2, 3]
        copy(km, kreg(k, order[0]), both=True)
        for m in order[1:]:
            tt(ki if m == order[-1] else km, kreg(k, m), km, A_.min)
        tsc(("MI%d" % k, 0, n), ki, SC - 1, None, A_.bitwise_and)
        tsc(("OU%d" % k, 0, n), ("MI%d" % k, 0, n), 16.0, ("PF", 0, 1), A_.mult, A_.add)
        ps = [a + n * q // NSP[k] for q in range(NSP[k] + 1)]
        cur[0] = "E%d" % k
        for x, y in zip(ps, ps[1:]):
            nr, win, off = ("NR", 16 * x, 16 * y), ("DA%d" % k, 0, 80 * n), ("OU%d" % k, x - a, y - a)
            cur[0] = "E%d%d" % (k, ps.index(x))
            if (k, ps.index(x)) in NEARS:
                gather(nr, win, off, "S")
                signdiff(nr, ("NW", 16 * x, 16 * y), nr)
            else:
                gather_tt(nr, win, off, ("NW", 16 * x, 16 * y), A_.is_lt)
            stage_sum(("CB", x, y), nr)
        dd = ("DD%d" % k, 0, n)
        cur[0] = "D%d" % k
        for m in range(5):
            r = kreg(k, m)
            tt(r, r, ki, A_.is_equal)
        tt((kb, 0, 4 * n), (kb, 0, 4 * n), ("CI%d" % k, 0, 4 * n), A_.mult)
        r = kreg(k, 4)
        tt(r, r, ("MN", a, b), A_.mult)
        tt(dd, (kb, 0, n), ("RN", a, b), A_.subtract)
        for m in range(1, 5):
            tt(dd, kreg(k, m), dd, A_.add)
        for x, y in zip(ps, ps[1:]):
            cur[0] = "P%d%d" % (k, ps.index(x))
            c = ("CB", x, y)
            tsc(c, c, (1.0 if (k, ps.index(x)) in NEARS else 8.5) * SC, None, A_.is_gt)
            tt(c, c, (dd[0], x - a, y - a), A_.mult)
            rp = ("RP", 8 + x, 8 + y)
            tt(rp, c, ("RN", x, y), A_.add)
            copy(("PU", x, y), rp)
            gather(("GP", 16 * x, 16 * y), XWIN, ("PU", x, y))

    def necks(na, nb, last):
        absdiff(("AB", 16 * na, 16 * nb), ("GP", 16 * na, 16 * nb), ("GP", 16 * na + 256, 16 * nb + 256))
        stage_sum(("NB", na, nb), ("AB", 16 * na, 16 * nb))
        tt(("DDN", na, nb), ("RP", 24 + na, 24 + nb), ("RP", 8 + na, 8 + nb), A_.subtract)
        hi = 255 if last else nb
        n = hi - na
        ini = ("RM", na - 1, na) if na else 1.0e7
        rd = [("NB", na, hi), ("BIGC", na, hi)] + ([ini] if na else [])
        O({"V": vt(n, 1)}, lambda e, g, T, op: g.vector.tensor_tensor_scan(T.RM[:, na:hi], T.NB[:, na:hi], T.BIGC[:, na:hi],
            sl(T, ini) if na else 1.0e7, A_.min, A_.min), rd, [("RM", na, hi)])
        tsc(("NB", 257 + na, 257 + hi), ("RM", na, hi), ("THR", 0, 1), None, A_.is_lt)

    def shift(ta, tb, last):
        m = ("NB", ta, tb)
        tt(m, ("NB", 256 + ta, 256 + tb), ("DDN", ta, tb), A_.mult)
        tt(("RN", ta, tb), m, ("RP", 8 + ta, 8 + tb), A_.add)
        copy(("RU", ta, tb), ("RN", ta, tb))

    def loops(t):
        O({"V": vt(256, 1)}, lambda e, g, T, op: g.vector.tensor_reduce(T.CNT[:], T.NB[:, 256:512], AxisListType.X, A_.add),
          [("NB", 256, 512)], [("CNT", 0, 1)])
        tsc(("OFF", 0, 16), ("IK", 0, 16), ("CNT", 0, 1), None, A_.subtract)
        gather_tt(("LG", 0, 256), ("RP", 8, 296), ("OFF", 0, 16), ("DIAG", 0, 256), A_.mult)
        O({"V": vt(256, 1)}, lambda e, g, T, op: g.vector.tensor_tensor_scan(T.LS[:], T.SEG[:], T.LG[:], 0.0, A_.mult, A_.add),
          [("SEG", 0, 256), ("LG", 0, 256)], [("LS", 0, 256)])
        s = "SEND%d" % t
        O({"V": vt(16, 1)}, lambda e, g, T, op: g.vector.tensor_scalar(T[s][:], T.LS[:, 15:256:16], 4096.0, None, A_.add),
          [("LS", 0, 256)], [(s, 0, 16)])
        snd = O({"G": 1500}, None, [(s, 0, 16)], [], send=t)
        tsc(("AC", 0, 1), ("NB", 511, 512), ("AC", 0, 1), None, A_.add)
        tsc(("THR", 0, 1), ("NB", 511, 512), 16.0 * SC, ("THR", 0, 1), A_.mult, A_.add)
        return snd

    def loop_in(t, snd, last):
        q = O({"V": vt(16, 2)}, lambda e, g, T, op: g.vector.tensor_tensor(T.LPI[:], T["LAND%d" % t][:], T.LS[:, 15:256:16], A_.max),
              [("LS", 0, 256)], [("LPI", 0, 16)], ext="arr%d" % t)
        q["preds"][snd["i"]] = 1
        tsc(("LPI", 0, 16), ("LPI", 0, 16), 4095, None, A_.bitwise_and)
        tt(("LD", 0, 16), ("LPI", 0, 16), ("RP", 248, 264), A_.subtract)
        tt(("LD", 0, 16), ("NB", 496, 512), ("LD", 0, 16), A_.mult)
        tt(("RN", 240, 256), ("LD", 0, 16), ("RP", 248, 264), A_.add)
        copy(("RU", 240, 256), ("RN", 240, 256))

    for i in range(NT):
        first_names(TB[i], TB[i + 1])
    copy(("MN", 0, 256), ("BI", 0, 256))
    copy(("MU", 0, 256), ("BI", 0, 256))
    copy(("EPF", 0, 1), ("EI", 0, 1))
    tsc(("THR", 0, 1), ("TI", 0, 1), float(SC), None, A_.mult)
    for t in range(RO):
        for i in range(NT):
            ta, tb = TB[i], TB[i + 1]
            cur[0] = "R%d" % i
            names_side(t, ta, tb, "R")
            if i >= NA - 1 and i < NT - 1:
                continue
            if i == NT - 1:
                ta = TB[NA - 1]
            if t:
                cur[0] = "A%d" % i
                accretion(ta, tb, False)
            cur[0] = "M%d" % i
            names_side(t, ta, tb, "M")
        for k in range(NCH):
            a, b = BND[k], BND[k + 1]
            cur[0] = "L%d0" % k
            cand_lists(k, 0)
            cur[0] = "L%d1" % k
            cand_lists(k, 1)
            hi = min(16 * b, 4080)
            for m in (4, 0, 1, 2, 3):
                cur[0] = "C%d%d" % (k, m)
                cand_heights(k, m)
            cur[0] = "N%d" % k
            absdiff(("NW", 16 * a, hi), ("GR", 16 * a, hi), ("GR", 16 * a + 16, hi + 16))
            choose(k)
            for q in range(NSP[k]):
                x, y = a + (b - a) * q // NSP[k], a + (b - a) * (q + 1) // NSP[k]
                cur[0] = "Q%d%d" % (k, q)
                if y == 256:
                    memset(("NB", 240, 255), 1.0e7)
                    memset(("NB", 256, 257), 0.0)
                necks(x - 16 if x else 0, y - 16, y == 256)
        cur[0] = "O"
        snd = loops(t)
        for i in range(NT - 1):
            cur[0] = "S%d" % i
            shift(TB[i], TB[i + 1], t == RO - 1)
        cur[0] = "I"
        loop_in(t, snd, t == RO - 1)
    for i in range(NT):
        ta, tb = TB[i], TB[i + 1]
        cur[0] = "FR%d" % i
        gather(("GR", 16 * ta, 16 * tb), XWIN, ("RU", ta, tb))
        cur[0] = "FA%d" % i
        accretion(ta, tb, True)

    def store(dst, src, w):
        O({"Y": 2000}, lambda e, g, T, op: g.sync.dma_start(T[dst][:], T[src][:, 0:w]), [(src, 0, w)], [], sem="st" + dst)
    store("ya", "AC", 1)
    store("yr", "RN", 256)
    store("ym", "MN", 256)
    return ops


def schedule(ops):
    n = len(ops)
    succ = [[] for _ in range(n)]
    left = [0] * n
    for op in ops:
        for p in op["preds"]:
            succ[p].append(op["i"])
            left[op["i"]] += 1
    prio = [0.0] * n
    free = {e: 0.0 for e in "VSPGY"}
    fin = [0.0] * n
    bank = {}
    pool = {b: None for b in POOL}
    ready = [i for i in range(n) if left[i] == 0]
    order = []
    choice = {}
    for op in ops:
        off, ch = TUNE.get(op["grp"], (0, "."))
        prio[op["i"]] = -(op["i"] + off)
        if len(op["engs"]) > 1 and ch in op["engs"] and max(op["engs"].values()) > 300:
            choice[op["i"]] = ch

    def done(i, f):
        fin[i] = f
        for q in succ[i]:
            left[q] -= 1
            if left[q] == 0:
                if ops[q].get("null"):
                    done(q, max([fin[p] for p in ops[q]["preds"]]))
                else:
                    ready.append(q)

    for op in ops:
        op["bk"] = sorted({r[0] for r in op["R"] + op["W"] if r[0] in PSUM})

    while ready:
        best = None
        found = []
        for i in ready:
            op = ops[i]
            t0 = 0.0
            for p in op["preds"]:
                x = fin[p] + LAT + (1500 if "send" in ops[p] else 0)
                t0 = max(t0, x)
            bk = None
            if op.get("alloc"):
                opts = [(fin[c] + LAT if c is not None else 0.0, b) for b, c in pool.items() if c != -1]
                if not opts:
                    continue
                x, bk = min(opts)
                t0 = max(t0, x)
            cand = None
            for e, d in op["engs"].items():
                if choice.get(i, e) != e:
                    continue
                s = max(t0, free[e])
                for b in op["bk"]:
                    for f, (x, q) in bank.get(b, {}).items():
                        if f != e:
                            s = max(s, x + LAT)
                if cand is None or s + d < cand[0]:
                    cand = (s + d, s, e)
            ef, s, e = cand
            found.append((s, i, e, ef, bk))
            if best is None or s < best[0]:
                best = found[-1]
        s0, e0 = best[0] + WIN, best[2]
        for x in found:
            if x[2] == e0 and x[0] <= s0 and prio[x[1]] > prio[best[1]]:
                best = x
        s, i, e, ef, bk = best
        op = ops[i]
        if "subs" in op and e == "V":
            for x in op["subs"] + op["abss"][1:]:
                ops[x]["null"] = True
            z = ops[op["abss"][0]]
            z["whole"] = True
            z["engs"] = {"S": z["wdur"]}
        ready.remove(i)
        op["eng"] = e
        op["deps"] = list(op["preds"])
        if op.get("alloc"):
            op["bank"] = bk
            if pool[bk] is not None:
                op["deps"].append(pool[bk])
            pool[bk] = -1
        if "src" in op and not op.get("whole"):
            pool[op["src"]["bank"]] = i
        for b in op["bk"]:
            d = bank.setdefault(b, {})
            for f, (x, q) in d.items():
                if f != e:
                    op["deps"].append(q)
            d[e] = (ef, i)
        op["start"] = s
        free[e] = s + 60.0 if e == "Y" else ef
        order.append(i)
        done(i, ef)
    return order, max(fin)


def make_plan():
    ops = build_ops()
    order, span = schedule(ops)
    know = {e: {} for e in "VSPGY"}
    cnt = {"V": 0, "S": 0, "P": 0, "G": 0}
    out = []
    for i in order:
        op = ops[i]
        e = op["eng"]
        need = {}
        srcs = []
        deps = list(op["deps"])
        for d in deps:
            q = ops[d]
            if q.get("null"):
                deps.extend(x for x in q["preds"] if x not in deps)
                continue
            if "send" in q:
                if "ext" in op:
                    need[op["ext"]] = "ARR"
                continue
            sem, v = q["tok"]
            if know[e].get(sem, 0) < v:
                srcs.append((v, sem, q))
        srcs.sort(key=lambda x: -x[2]["pos"])
        for v, sem, q in srcs:
            if know[e].get(sem, 0) >= v:
                continue
            need[sem] = max(need.get(sem, 0), v)
            know[e][sem] = v
            for s2, v2 in q["clk"].items():
                if know[e].get(s2, 0) < v2:
                    know[e][s2] = v2
        op["waits"] = need
        op["clk"] = dict(know[e])
        op["pos"] = len(out)
        if "sem" in op:
            op["tok"] = (op["sem"], 16)
        elif "send" in op:
            op["tok"] = None
        else:
            cnt[e] += 1
            op["tok"] = ("q" + e, cnt[e])
        out.append(op)
    return out, cnt, span


CACHE = {}


def rank_program(g, core, T, topo):
    rank = T.rank_of(core)
    if rank is None:
        return
    if "plan" not in CACHE:
        CACHE["plan"] = make_plan()
    plan, cnt, span = CACHE["plan"]
    N = len(T.cores)
    hand = {"V": g.vector, "S": g.scalar, "P": g.tensor, "G": g, "Y": g.sync}

    def link(src, dst):
        return topo.engines(src, dst)[:4]

    for op in plan:
        e = op["eng"]
        h = hand[e]
        for sem, v in op["waits"].items():
            if v == "ARR":
                t = int(sem[3:])
                v = len(link(T.cores[(rank - 1 - t % (N - 1)) % N], core))
            h.wait_ge(T.sem[sem], v)
        if "send" in op:
            t = op["send"]
            dst = T.cores[(rank + 1 + t % (N - 1)) % N]
            rid, pid, _s = topo.addr(dst)
            mask = 0
            for x in link(core, dst):
                mask |= 1 << x
            g.remote_dma(T["LAND%d" % t][:], T["SEND%d" % t][:], T.sem["arr%d" % t], T.sem["snt%d" % t], pid, rid, mask)
            continue
        ins = op["fn"](e, g, T, op)
        sem, v = op["tok"]
        ins.then_inc(T.sem[sem], 16 if "sem" in op else 1)
    for t in range(RO):
        g.wait_ge(T.sem["snt%d" % t], len(link(core, T.cores[(rank + 1 + t % (N - 1)) % N])))
    for e in "VSPG":
        g.wait_ge(T.sem["q" + e], cnt[e])
    for n in LOADS:
        g.sync.wait_ge(T.sem["ld" + n], 16)
    for n in OUTS:
        g.sync.wait_ge(T.sem["st" + n], 16)
